import numpy as np
import ml_dtypes


def mxq(x, axis, fmt="e4m3"):
    dtype, down = {"e4m3": (ml_dtypes.float8_e4m3fn, 7), "e5m2": (ml_dtypes.float8_e5m2, 14)}[fmt]
    v = np.moveaxis(np.asarray(x, np.float32).astype(ml_dtypes.bfloat16).astype(np.float64), axis, -1)
    blocks = v.reshape(v.shape[:-1] + (-1, 32))
    amax = np.abs(blocks).max(-1, keepdims=True)
    byte = np.maximum(np.where(amax > 0, np.frexp(amax)[1] - 1 + 127, 0) - down, 1)
    scale = np.exp2(byte - 127.0)
    codes = (blocks / scale).astype(np.float32).astype(dtype).astype(np.float64)
    return np.moveaxis((codes * scale).reshape(v.shape), -1, axis)


WIDE = False


def mx_kscale(k):
    if not WIDE:
        return np.ones(k)
    levels = np.array([10, -10, 5, -5, 0])
    if k % 512:
        return np.exp2(np.random.permutation(np.resize(levels, k // 32))).repeat(32)
    a = np.empty((k // 512, 16))
    for p in range(k // 512):
        a[p, :8] = np.random.permutation(np.resize(levels, 8))
        for g in range(8):
            far = levels[np.abs(levels - a[p, g]) >= 10]
            a[p, g + 8] = far[np.random.randint(len(far))]
    return np.exp2(a.ravel()).repeat(32)


def f64(x):
    return np.asarray(x).astype(np.float64)


def striped8(idx):
    return np.asarray(idx).reshape(8, -1, 16).transpose(0, 2, 1).reshape(128, -1).astype(np.uint16)


def unstriped8(offs):
    return offs.reshape(8, 16, -1).transpose(0, 2, 1).reshape(8, -1).astype(np.int64)


def pick8(x, idx, run):
    r = np.arange(len(x))
    return x[r[:, None], idx[r % (8 * run) // run]]


E2M1 = np.array([0.0, 0.5, 1.0, 1.5, 2.0, 3.0, 4.0, 6.0, -0.0, -0.5, -1.0, -1.5, -2.0, -3.0, -4.0, -6.0])


def pack_weight(w, fmt):
    k, n = w.shape
    w = f64(np.asarray(w, np.float32).astype(ml_dtypes.bfloat16)).reshape(k // 32, 32, n)
    amax = np.abs(w).max(1)
    if fmt == "e4m3":
        byte = np.frexp(amax)[1] - 1 + 127 - 7
    else:
        mant, ex = np.frexp(amax / 6.0)
        byte = np.where(mant > 0.5, ex, ex - 1) + 127
    byte = np.clip(np.where(amax > 0, byte, 1), 1, 254)
    scaled = (w * np.exp2(127.0 - byte)[:, None, :]).reshape(k, n).astype(np.float32)
    by_word = np.ascontiguousarray(scaled.reshape(k // 512, 128, 4, n).transpose(0, 1, 3, 2))
    if fmt == "e4m3":
        words = by_word.astype(ml_dtypes.float8_e4m3fn).view(np.uint8)
    else:
        c = by_word.astype(ml_dtypes.float4_e2m1fn).view(np.uint8) & 0xF
        words = (c[..., 0::2] | (c[..., 1::2] << 4)).reshape(k // 512, 128, 2 * n)
    return np.ascontiguousarray(words), np.ascontiguousarray(byte.astype(np.uint8).reshape(k // 512, 16, n))


def unpack_weight(words, scales, fmt):
    g, _, n = scales.shape
    words = np.ascontiguousarray(words).reshape(g, 128, n, -1)
    if fmt == "e4m3":
        vals = words.view(ml_dtypes.float8_e4m3fn).astype(np.float64)
    else:
        nib = np.empty((g, 128, n, 4), np.uint8)
        nib[..., 0::2] = words & 0xF
        nib[..., 1::2] = words >> 4
        vals = E2M1[nib]
    vals = vals * np.repeat(np.exp2(scales.astype(np.float64) - 127.0), 8, axis=1)[..., None]
    return vals.transpose(0, 1, 3, 2).reshape(g * 512, n)


def sigmoid(v):
    return 1.0 / (1.0 + np.exp(-v))


D, V, Q, I = 512, 2048, 128, 512


def setup_inputs():
    n = np.random.standard_normal
    idx = np.stack([np.random.permutation(V)[:I] for _ in range(8)])
    idx2 = np.stack([np.random.permutation(V)[:I] for _ in range(8)])
    fd = mx_kscale(D)
    vocp = pack_weight(n((D, V)) / fd[:, None], "e4m3")
    return {
        "hid": (n((D, Q)) * 1.0 / np.sqrt(D) * fd[:, None]).astype(np.float32),
        "voc_words": vocp[0],
        "voc_scales": vocp[1],
        "sw": (np.random.uniform(0.5, 2.0, (1, I))).astype(np.float32),
        "sw2": (np.random.uniform(0.5, 2.0, (1, I))).astype(np.float32),
        "saved": (np.random.uniform(-0.5, 0.5, (Q, 1))).astype(np.float32),
        "beta": (np.random.uniform(1.0, 3.0, (Q, 1))).astype(np.float32),
        "dhid": (n((D, Q)) * 1.0 / np.sqrt(D) * fd[:, None]).astype(np.float32),
        "base": (0.5 * n((Q, V))).astype(np.float32),
        "offs": striped8(idx),
        "offs2": striped8(idx2),
    }


def reference(hid, voc_words, voc_scales, sw, sw2, saved, beta, dhid, base, offs, offs2):
    idx = unstriped8(offs)
    idx2 = unstriped8(offs2)
    vocu = unpack_weight(voc_words, voc_scales, "e4m3")
    hidq = mxq(f64(hid), 0, "e4m3")
    a = hidq.T @ vocu
    dhidq = mxq(f64(dhid), 0, "e4m3")
    ta = dhidq.T @ vocu
    m1 = np.max(a, axis=1, keepdims=True)
    px = np.exp(pick8(a, idx, 16) - m1)
    px2 = np.exp(pick8(a, idx2, 16) - m1)
    s1l = np.sum(px * f64(sw), axis=1, keepdims=True)
    s2l = np.sum(px2 * f64(sw2), axis=1, keepdims=True)
    dl = np.log(s1l) - np.log(s2l) - f64(saved)
    ddl = sigmoid(dl * f64(beta) * (-1.0)) * f64(beta)
    ds2l = ddl * (-1.0) / s2l
    ds1l = ddl / s1l
    dpx2 = ds2l * f64(sw2)
    dpx = ds1l * f64(sw)
    xpx = pick8(ta, idx, 16) * px
    xpx2 = pick8(ta, idx2, 16) * px2
    xs1l = np.sum(xpx * f64(sw), axis=1, keepdims=True)
    xs2l = np.sum(xpx2 * f64(sw2), axis=1, keepdims=True)
    xdl = xs1l / s1l - xs2l / s2l
    xddl = xdl * f64(beta) * (-1.0) * sigmoid(dl * f64(beta) * (-1.0)) * (1.0 - sigmoid(dl * f64(beta) * (-1.0))) * f64(beta)
    xds2l = (xddl * (-1.0) - xs2l * ddl * (-1.0) / s2l) / s2l
    xds1l = (xddl - xs1l * ddl / s1l) / s1l
    xdpx2 = xds2l * f64(sw2)
    xdpx = xds1l * f64(sw)
    xe1 = xdpx2 * px2 + xpx2 * dpx2
    xs1 = np.zeros((Q, V))
    xs1[np.arange(Q)[:, None], idx2[np.arange(Q) % 128 // 16]] = xe1
    xe2 = xdpx * px + xpx * dpx
    xs2 = np.zeros((Q, V))
    xs2[np.arange(Q)[:, None], idx[np.arange(Q) % 128 // 16]] = xe2
    xda = xs1 + xs2
    y = xda * 256.0 + f64(base)
    return y

@@ -1,0 +1,225 @@
+from contextlib import ExitStack
+
+import concourse.mybir as mybir
+from concourse.masks import make_identity
+
+D, V, Q, I = 512, 2048, 128, 512
+FLOPS = 2 * 2 * D * V * Q
+
+F32 = mybir.dt.float32
+BF16 = mybir.dt.bfloat16
+I32 = mybir.dt.int32
+U32 = mybir.dt.uint32
+U16 = mybir.dt.uint16
+U8 = mybir.dt.uint8
+FP8X4 = mybir.dt.float8_e4m3fn_x4
+ALU = mybir.AluOpType
+ACT = mybir.ActivationFunctionType
+AX = mybir.AxisListType
+
+P = 128
+PACK = 4
+N = 512
+CHUNKS = V // N
+BLOCKS = N // P
+OUT_SCALE = 256.0
+W_CAP = 1e30
+WORD_LOADS = ((0, 2), (2, 3), (3, 4))
+
+
+def tile_attend_hvodds_heads_kernel(tc, hid, voc_words, voc_scales, sw, sw2, saved, beta, dhid, base, offs, offs2, out):
+    nc = tc.nc
+    with ExitStack() as ctx:
+        sb = ctx.enter_context(tc.tile_pool(name="sb", bufs=1))
+        psum = ctx.enter_context(tc.psum_pool(name="psum", bufs=1))
+
+        planes = sb.tile([P, N], U8, name="planes", align_bytes=64)
+        nc.vector.memset(planes[:].bitcast(I32), 0)
+        for quad in range(4):
+            nc.scalar.dma_start(
+                out=planes[32 * quad : 32 * quad + 16, :].bitcast(I32),
+                in_=voc_scales[0, 4 * quad : 4 * quad + 4, :].rearrange("r (c n) -> c r n", c=CHUNKS).bitcast(I32),
+            )
+
+        raw = [sb.tile([P, PACK, Q], F32, name="raw%d" % k) for k in range(2)]
+        nc.sync.dma_start(out=raw[0][:], in_=hid.rearrange("(p j) q -> p j q", j=PACK))
+        words_flat = voc_words[0].rearrange("p n t -> p (n t)")
+        words = []
+        for first, last in WORD_LOADS:
+            t = sb.tile([P, (last - first) * N], U32, name="words%d" % first, align_bytes=64)
+            nc.sync.dma_start(out=t[:].bitcast(I32), in_=words_flat[:, PACK * N * first : PACK * N * last].bitcast(I32))
+            for c in range(last - first):
+                words.append(t[:, c * N : (c + 1) * N])
+        nc.sync.dma_start(out=raw[1][:], in_=dhid.rearrange("(p j) q -> p j q", j=PACK))
+        lists = []
+        for name, src in (("list1", offs), ("list2", offs2)):
+            t = sb.tile([P, I // 16], U16, name=name)
+            nc.sync.dma_start(t[:], src)
+            lists.append(t)
+        saved_t = sb.tile([P, 1], F32, name="saved_t")
+        nc.gpsimd.dma_start(out=saved_t[:], in_=saved)
+        beta_t = sb.tile([P, 1], F32, name="beta_t")
+        nc.gpsimd.dma_start(out=beta_t[:], in_=beta)
+        weights = []
+        for name, src in (("sw1", sw), ("sw2", sw2)):
+            t = sb.tile([P, I], F32, name=name)
+            nc.sync.dma_start(out=t[:], in_=src[0].partition_broadcast(P))
+            weights.append(t)
+        base_t = sb.tile([P, V], F32, name="base_t")
+        nc.sync.dma_start(out=base_t[:], in_=base)
+
+        ident = sb.tile([P, P], F32, name="ident")
+        make_identity(nc, ident[:])
+        one_zero = sb.tile([P, 2], F32, name="one_zero")
+        nc.gpsimd.memset(one_zero[:, 0:1], 1.0)
+        nc.gpsimd.memset(one_zero[:, 1:2], 0.0)
+
+        exp_saved = sb.tile([P, 1], F32, name="exp_saved")
+        nc.scalar.activation(exp_saved[:], saved_t[:], ACT.Exp)
+
+        def quantise(k, engine_copy):
+            grouped = sb.tile([P, Q, PACK], BF16, name="grouped%d" % k, align_bytes=64)
+            engine_copy(out=grouped[:], in_=raw[k][:].rearrange("p j q -> p q j"))
+            cw = sb.tile([P, Q], U32, name="codes%d" % k, align_bytes=64)
+            sc = sb.tile([P, Q], U8, name="scales%d" % k, align_bytes=64)
+            nc.vector.quantize_mx(out=cw[:].bitcast(FP8X4), scales=sc[:], in_=grouped[:].rearrange("p q j -> p (q j)"))
+            return cw, sc
+
+        def score(cw, sc, c, tag):
+            bank = psum.tile([P, N], F32, name="score_" + tag, tag=tag)
+            nc.tensor.matmul_mx(
+                out=bank[:],
+                lhsT=cw[:].bitcast(FP8X4),
+                lhsT_scale=sc[:],
+                rhs=words[c].bitcast(FP8X4),
+                rhs_scale=planes[4 * c : P, :],
+                start=True,
+                stop=True,
+            )
+            return bank
+
+        a = sb.tile([P, V], F32, name="a")
+        ta = sb.tile([P, V], F32, name="ta")
+        chunk_max = sb.tile([P, CHUNKS], F32, name="chunk_max")
+        cw, sc = quantise(0, nc.vector.tensor_copy)
+        for c in range(CHUNKS):
+            bank = score(cw, sc, c, "low%d" % c)
+            nc.vector.tensor_scalar(
+                out=a[:, c * N : (c + 1) * N], in0=bank[:], scalar1=1.0, scalar2=None, op0=ALU.mult, op1=ALU.max,
+                accum_out=chunk_max[:, c : c + 1],
+            )
+        cw, sc = quantise(1, nc.scalar.copy)
+        neg_max = sb.tile([P, 1], F32, name="neg_max")
+        nc.vector.tensor_reduce(out=neg_max[:], in_=chunk_max[:], axis=AX.X, op=ALU.max, negate=True)
+
+        px = []
+        for k in range(2):
+            picked = sb.tile([P, I], F32, name="picked%d" % k)
+            nc.vector.tensor_copy(picked[:], a[:].indirect(lists[k][:]))
+            e = sb.tile([P, I], F32, name="px%d" % k)
+            nc.scalar.activation(e[:], picked[:], ACT.Exp, bias=neg_max[:])
+            px.append(e)
+        for c in range(CHUNKS):
+            bank = score(cw, sc, c, "high%d" % c)
+            nc.scalar.copy(out=ta[:, c * N : (c + 1) * N], in_=bank[:])
+
+        sums = sb.tile([P, 2], F32, name="sums")
+        ew = []
+        for k in range(2):
+            e = sb.tile([P, I], F32, name="ew%d" % k)
+            nc.vector.scalar_tensor_tensor(e[:], px[k][:], 1.0, weights[k][:], ALU.mult, ALU.mult, accum_out=sums[:, k : k + 1])
+            ew.append(e)
+        inv = sb.tile([P, 2], F32, name="inv")
+        nc.vector.reciprocal(inv[:], sums[:])
+
+        def column(name, width=1):
+            return sb.tile([P, width], F32, name=name)
+
+        odds = column("odds")
+        nc.gpsimd.tensor_scalar(odds[:], sums[:, 1:2], inv[:, 0:1], exp_saved[:], ALU.mult, ALU.mult)
+        power = column("power")
+        nc.gpsimd.tensor_tensor(power[:], odds[:], beta_t[:], ALU.pow)
+        den = column("den")
+        nc.gpsimd.tensor_scalar(den[:], power[:], W_CAP, 1.0, ALU.min, ALU.add)
+        capped = column("capped")
+        nc.gpsimd.tensor_scalar(capped[:], power[:], W_CAP, OUT_SCALE, ALU.min, ALU.mult)
+
+        tg = [sb.tile([P, I], F32, name="tg%d" % k) for k in range(2)]
+        xsums = [column("xsum%d" % k) for k in range(2)]
+        xw = sb.tile([P, I], F32, name="xw")
+        nc.vector.tensor_copy(tg[0][:], ta[:].indirect(lists[0][:]))
+        rest = column("rest")
+        nc.vector.reciprocal(rest[:], den[:])
+        nc.vector.scalar_tensor_tensor(xw[:], tg[0][:], 1.0, ew[0][:], ALU.mult, ALU.mult, accum_out=xsums[0][:])
+        nc.vector.tensor_copy(tg[1][:], ta[:].indirect(lists[1][:]))
+        nc.vector.scalar_tensor_tensor(xw[:], tg[1][:], 1.0, ew[1][:], ALU.mult, ALU.mult, accum_out=xsums[1][:])
+
+        slope = column("slope")
+        nc.scalar.activation(slope[:], rest[:], ACT.Copy, scale=beta_t[:])
+        mix1 = column("mix1", 2)
+        nc.scalar.activation(mix1[:], one_zero[:], ACT.Identity, bias=slope[:])
+        grad = column("grad")
+        nc.scalar.activation(grad[:], capped[:], ACT.Copy, scale=slope[:])
+        mix2 = column("mix2", 2)
+        nc.scalar.activation(mix2[:], mix1[:], ACT.Identity, scale=-1.0, bias=1.0)
+        mean1 = column("mean1")
+        nc.scalar.activation(mean1[:], xsums[0][:], ACT.Copy, scale=inv[:, 0:1])
+        factor = column("factor", 2)
+        nc.scalar.activation(factor[:], inv[:], ACT.Copy, scale=grad[:])
+        per_x2 = column("per_x2", 2)
+        nc.scalar.activation(per_x2[:], mix2[:], ACT.Copy, scale=inv[:, 1:2])
+        from_x1 = column("from_x1", 2)
+        nc.scalar.activation(from_x1[:], mix1[:], ACT.Copy, scale=mean1[:])
+        neg_factor2 = column("neg_factor2")
+        nc.scalar.activation(neg_factor2[:], factor[:, 1:2], ACT.Copy, scale=-1.0)
+        centre = column("centre", 2)
+        nc.vector.scalar_tensor_tensor(centre[:], per_x2[:], xsums[1][:], from_x1[:], ALU.mult, ALU.add)
+
+        placed = [sb.tile([P, V], F32, name="placed%d" % k) for k in range(2)]
+        for k in range(2):
+            for c in range(CHUNKS):
+                nc.vector.memset(placed[k][:, c * N : (c + 1) * N], 0.0)
+
+        turned = []
+        for c in range(CHUNKS):
+            bank = psum.tile([P, BLOCKS, P], F32, name="turned%d" % c, tag="low%d" % c)
+            for b in range(BLOCKS):
+                cols = slice(c * N + b * P, c * N + (b + 1) * P)
+                nc.tensor.matmul(bank[:, b, :], base_t[:, cols], ident[:], start=(b == 0), stop=False, is_transpose=True)
+            turned.append(bank)
+
+        h = [sb.tile([P, I], F32, name="h%d" % k) for k in range(2)]
+        nc.vector.tensor_scalar(h[0][:], tg[0][:], centre[:, 0:1], factor[:, 0:1], ALU.subtract, ALU.mult)
+        nc.vector.tensor_tensor(placed[0][:].indirect(lists[0][:]), ew[0][:], h[0][:], ALU.mult)
+        shift2 = column("shift2")
+        nc.scalar.activation(shift2[:], centre[:, 1:2], ACT.Copy, scale=factor[:, 1:2])
+        nc.scalar.activation(h[1][:], tg[1][:], ACT.Identity, scale=neg_factor2[:], bias=shift2[:])
+        nc.vector.tensor_tensor(placed[1][:].indirect(lists[1][:]), ew[1][:], h[1][:], ALU.mult)
+
+        staged = []
+        partial = []
+
+        def turn_back(c):
+            bank = psum.tile([P, BLOCKS, P], F32, name="partial%d" % c, tag="high%d" % c)
+            for b in range(BLOCKS):
+                nc.tensor.transpose(bank[:, b, :], staged[c][:, b, :], ident[:])
+            partial.append(bank)
+
+        for c in range(CHUNKS):
+            for b in range(BLOCKS):
+                cols = slice(c * N + b * P, c * N + (b + 1) * P)
+                nc.tensor.matmul(
+                    turned[c][:, b, :], placed[0][:, cols], ident[:], start=False, stop=(b == BLOCKS - 1), is_transpose=True
+                )
+            t = sb.tile([P, BLOCKS, P], F32, name="staged%d" % c)
+            nc.scalar.copy(out=t[:], in_=turned[c][:])
+            staged.append(t)
+            if c > 0:
+                turn_back(c - 1)
+        turn_back(CHUNKS - 1)
+
+        for c in range(CHUNKS):
+            cols = slice(c * N, (c + 1) * N)
+            res = sb.tile([P, N], F32, name="res%d" % c)
+            nc.vector.tensor_tensor(res[:], partial[c][:].rearrange("p b v -> p (b v)"), placed[1][:, cols], ALU.add)
+            nc.sync.dma_start(out=out[:, cols], in_=res[:])

@@ -24,7 +24,8 @@ CHUNKS = V // N
 BLOCKS = N // P
 OUT_SCALE = 256.0
 W_CAP = 1e30
-WORD_LOADS = ((0, 2), (2, 3), (3, 4))
+TA_BANKS = ("high0", "high1", "low0", "low1")
+OUT_PIECES = ((0, 512), (512, 1024), (1024, 1536), (1536, 1792), (1792, 2048))
 
 
 def tile_attend_hvodds_heads_kernel(tc, hid, voc_words, voc_scales, sw, sw2, saved, beta, dhid, base, offs, offs2, out):
@@ -33,53 +34,64 @@ def tile_attend_hvodds_heads_kernel(tc, hid, voc_words, voc_scales, sw, sw2, sav
         sb = ctx.enter_context(tc.tile_pool(name="sb", bufs=1))
         psum = ctx.enter_context(tc.psum_pool(name="psum", bufs=1))
 
-        planes = sb.tile([P, N], U8, name="planes", align_bytes=64)
-        nc.vector.memset(planes[:].bitcast(I32), 0)
-        for quad in range(4):
-            nc.scalar.dma_start(
-                out=planes[32 * quad : 32 * quad + 16, :].bitcast(I32),
-                in_=voc_scales[0, 4 * quad : 4 * quad + 4, :].rearrange("r (c n) -> c r n", c=CHUNKS).bitcast(I32),
-            )
+        def column(name, width=1):
+            return sb.tile([P, width], F32, name=name)
+
+        zero_one = column("zero_one", 2)
+        nc.gpsimd.memset(zero_one[:, 0:1], 0.0)
+        nc.gpsimd.memset(zero_one[:, 1:2], 1.0)
+        signs = column("signs", 2)
+        nc.scalar.activation(signs[:], zero_one[:], ACT.Identity, scale=-2.0, bias=1.0)
 
         raw = [sb.tile([P, PACK, Q], F32, name="raw%d" % k) for k in range(2)]
         nc.sync.dma_start(out=raw[0][:], in_=hid.rearrange("(p j) q -> p j q", j=PACK))
+        landed = sb.tile([P, N // 4], I32, name="landed")
+        for quad in range(4):
+            queue = nc.gpsimd if quad < 2 else nc.sync
+            queue.dma_start(
+                out=landed[32 * quad : 32 * quad + 16, :],
+                in_=voc_scales[0, 4 * quad : 4 * quad + 4, :].rearrange("r (c n) -> c r n", c=CHUNKS).bitcast(I32),
+            )
+        planes = sb.tile([P, N], U8, name="planes", align_bytes=64)
+        nc.vector.memset(planes[:].bitcast(I32), 0)
+        placed = [sb.tile([P, V], F32, name="placed%d" % k) for k in range(2)]
+        for k in range(2):
+            for c in range(CHUNKS):
+                nc.vector.memset(placed[k][:, c * N : (c + 1) * N].bitcast(I32), 0)
         words_flat = voc_words[0].rearrange("p n t -> p (n t)")
         words = []
-        for first, last in WORD_LOADS:
-            t = sb.tile([P, (last - first) * N], U32, name="words%d" % first, align_bytes=64)
-            nc.sync.dma_start(out=t[:].bitcast(I32), in_=words_flat[:, PACK * N * first : PACK * N * last].bitcast(I32))
-            for c in range(last - first):
-                words.append(t[:, c * N : (c + 1) * N])
-        nc.sync.dma_start(out=raw[1][:], in_=dhid.rearrange("(p j) q -> p j q", j=PACK))
+        for c in range(CHUNKS):
+            t = sb.tile([P, N], U32, name="words%d" % c, align_bytes=64)
+            nc.sync.dma_start(out=t[:].bitcast(I32), in_=words_flat[:, PACK * N * c : PACK * N * (c + 1)].bitcast(I32))
+            words.append(t[:])
+            if c == 0:
+                nc.sync.dma_start(out=raw[1][:], in_=dhid.rearrange("(p j) q -> p j q", j=PACK))
         lists = []
         for name, src in (("list1", offs), ("list2", offs2)):
             t = sb.tile([P, I // 16], U16, name=name)
             nc.sync.dma_start(t[:], src)
             lists.append(t)
-        saved_t = sb.tile([P, 1], F32, name="saved_t")
-        nc.gpsimd.dma_start(out=saved_t[:], in_=saved)
-        beta_t = sb.tile([P, 1], F32, name="beta_t")
-        nc.gpsimd.dma_start(out=beta_t[:], in_=beta)
-        weights = []
-        for name, src in (("sw1", sw), ("sw2", sw2)):
-            t = sb.tile([P, I], F32, name=name)
-            nc.sync.dma_start(out=t[:], in_=src[0].partition_broadcast(P))
-            weights.append(t)
+        slot_weights = []
+        for k, src in enumerate((sw, sw2)):
+            t = column("slot_weights%d" % k, BLOCKS)
+            nc.sync.dma_start(out=t[:], in_=src[0].rearrange("(n c) -> n c", c=BLOCKS))
+            slot_weights.append(t)
+        saved_t = column("saved_t")
+        nc.sync.dma_start(out=saved_t[:], in_=saved)
+        beta_t = column("beta_t")
+        nc.sync.dma_start(out=beta_t[:], in_=beta)
         base_t = sb.tile([P, V], F32, name="base_t")
         nc.sync.dma_start(out=base_t[:], in_=base)
 
         ident = sb.tile([P, P], F32, name="ident")
         make_identity(nc, ident[:])
-        one_zero = sb.tile([P, 2], F32, name="one_zero")
-        nc.gpsimd.memset(one_zero[:, 0:1], 1.0)
-        nc.gpsimd.memset(one_zero[:, 1:2], 0.0)
 
-        exp_saved = sb.tile([P, 1], F32, name="exp_saved")
-        nc.scalar.activation(exp_saved[:], saved_t[:], ACT.Exp)
-
-        def quantise(k, engine_copy):
+        def interleave(k, engine_copy):
             grouped = sb.tile([P, Q, PACK], BF16, name="grouped%d" % k, align_bytes=64)
             engine_copy(out=grouped[:], in_=raw[k][:].rearrange("p j q -> p q j"))
+            return grouped
+
+        def quantise(k, grouped):
             cw = sb.tile([P, Q], U32, name="codes%d" % k, align_bytes=64)
             sc = sb.tile([P, Q], U8, name="scales%d" % k, align_bytes=64)
             nc.vector.quantize_mx(out=cw[:].bitcast(FP8X4), scales=sc[:], in_=grouped[:].rearrange("p q j -> p (q j)"))
@@ -101,84 +113,94 @@ def tile_attend_hvodds_heads_kernel(tc, hid, voc_words, voc_scales, sw, sw2, sav
         a = sb.tile([P, V], F32, name="a")
         ta = sb.tile([P, V], F32, name="ta")
         chunk_max = sb.tile([P, CHUNKS], F32, name="chunk_max")
-        cw, sc = quantise(0, nc.vector.tensor_copy)
+        grouped = [interleave(0, nc.vector.tensor_copy), interleave(1, nc.scalar.copy)]
+        for quad in range(4):
+            rows = slice(32 * quad, 32 * quad + 16)
+            nc.vector.tensor_copy(out=planes[rows, :].bitcast(I32), in_=landed[rows, :])
+        quantised = [quantise(k, grouped[k]) for k in range(2)]
         for c in range(CHUNKS):
-            bank = score(cw, sc, c, "low%d" % c)
+            bank = score(*quantised[0], c, "low%d" % c)
             nc.vector.tensor_scalar(
                 out=a[:, c * N : (c + 1) * N], in0=bank[:], scalar1=1.0, scalar2=None, op0=ALU.mult, op1=ALU.max,
                 accum_out=chunk_max[:, c : c + 1],
             )
-        cw, sc = quantise(1, nc.scalar.copy)
+        for c in range(CHUNKS):
+            bank = score(*quantised[1], c, TA_BANKS[c])
+            nc.scalar.copy(out=ta[:, c * N : (c + 1) * N], in_=bank[:])
+        weights = []
+        for k in range(2):
+            bank = psum.tile([P, BLOCKS, P], F32, name="spread%d" % k, tag="high%d" % (2 + k))
+            for b in range(BLOCKS):
+                nc.tensor.transpose(bank[:, b, :], slot_weights[k][:, b : b + 1].to_broadcast([P, P]), ident[:])
+            weights.append(bank[:].rearrange("p c n -> p n c"))
         neg_max = sb.tile([P, 1], F32, name="neg_max")
         nc.vector.tensor_reduce(out=neg_max[:], in_=chunk_max[:], axis=AX.X, op=ALU.max, negate=True)
 
-        px = []
+        pair = sb.tile([P, 2, I], F32, name="px", tag="pair")
+        px = [pair[:, k, :] for k in range(2)]
         for k in range(2):
             picked = sb.tile([P, I], F32, name="picked%d" % k)
             nc.vector.tensor_copy(picked[:], a[:].indirect(lists[k][:]))
-            e = sb.tile([P, I], F32, name="px%d" % k)
-            nc.scalar.activation(e[:], picked[:], ACT.Exp, bias=neg_max[:])
-            px.append(e)
-        for c in range(CHUNKS):
-            bank = score(cw, sc, c, "high%d" % c)
-            nc.scalar.copy(out=ta[:, c * N : (c + 1) * N], in_=bank[:])
+            nc.scalar.activation(px[k], picked[:], ACT.Exp, bias=neg_max[:])
 
-        sums = sb.tile([P, 2], F32, name="sums")
+        exp_saved = column("exp_saved")
+        nc.scalar.activation(exp_saved[:], saved_t[:], ACT.Exp)
+        betas = column("betas", 2)
+        nc.scalar.activation(betas[:], signs[:], ACT.Copy, scale=beta_t[:])
+        beta_out = column("beta_out")
+        nc.scalar.activation(beta_out[:], beta_t[:], ACT.Copy, scale=OUT_SCALE)
+
+        sums = column("sums", 2)
         ew = []
         for k in range(2):
             e = sb.tile([P, I], F32, name="ew%d" % k)
-            nc.vector.scalar_tensor_tensor(e[:], px[k][:], 1.0, weights[k][:], ALU.mult, ALU.mult, accum_out=sums[:, k : k + 1])
+            nc.vector.scalar_tensor_tensor(
+                e[:].rearrange("p (n c) -> p n c", c=BLOCKS), px[k].rearrange("p (n c) -> p n c", c=BLOCKS), 1.0, weights[k],
+                ALU.mult, ALU.mult, accum_out=sums[:, k : k + 1],
+            )
             ew.append(e)
-        inv = sb.tile([P, 2], F32, name="inv")
+        inv = column("inv", 2)
         nc.vector.reciprocal(inv[:], sums[:])
 
-        def column(name, width=1):
-            return sb.tile([P, width], F32, name=name)
+        lifted = column("lifted", 2)
+        nc.scalar.activation(lifted[:], sums[:, 1:2].to_broadcast([P, 2]), ACT.Copy, scale=exp_saved[:])
+        odds = column("odds", 2)
+        nc.scalar.activation(odds[:], lifted[:], ACT.Copy, scale=inv[:, 0:1])
+        powers = column("powers", 2)
+        nc.gpsimd.tensor_tensor(powers[:], odds[:], betas[:], ALU.pow)
+        gain = column("gain", 2)
+        nc.scalar.activation(gain[:, 0:1], inv[:, 0:1], ACT.Copy, scale=beta_out[:])
+        neg_beta_inv2 = column("neg_beta_inv2")
+        nc.scalar.activation(neg_beta_inv2[:], inv[:, 1:2], ACT.Copy, scale=betas[:, 1:2])
+        nc.scalar.activation(gain[:, 1:2], neg_beta_inv2[:], ACT.Copy, scale=OUT_SCALE)
+        den = column("den", 2)
+        nc.scalar.activation(den[:], powers[:], ACT.Identity, bias=1.0)
 
-        odds = column("odds")
-        nc.gpsimd.tensor_scalar(odds[:], sums[:, 1:2], inv[:, 0:1], exp_saved[:], ALU.mult, ALU.mult)
-        power = column("power")
-        nc.gpsimd.tensor_tensor(power[:], odds[:], beta_t[:], ALU.pow)
-        den = column("den")
-        nc.gpsimd.tensor_scalar(den[:], power[:], W_CAP, 1.0, ALU.min, ALU.add)
-        capped = column("capped")
-        nc.gpsimd.tensor_scalar(capped[:], power[:], W_CAP, OUT_SCALE, ALU.min, ALU.mult)
-
-        tg = [sb.tile([P, I], F32, name="tg%d" % k) for k in range(2)]
+        pair = sb.tile([P, 2, I], F32, name="tg", tag="pair")
+        tg = [pair[:, k, :] for k in range(2)]
         xsums = [column("xsum%d" % k) for k in range(2)]
-        xw = sb.tile([P, I], F32, name="xw")
-        nc.vector.tensor_copy(tg[0][:], ta[:].indirect(lists[0][:]))
-        rest = column("rest")
-        nc.vector.reciprocal(rest[:], den[:])
-        nc.vector.scalar_tensor_tensor(xw[:], tg[0][:], 1.0, ew[0][:], ALU.mult, ALU.mult, accum_out=xsums[0][:])
-        nc.vector.tensor_copy(tg[1][:], ta[:].indirect(lists[1][:]))
-        nc.vector.scalar_tensor_tensor(xw[:], tg[1][:], 1.0, ew[1][:], ALU.mult, ALU.mult, accum_out=xsums[1][:])
+        xw = [sb.tile([P, I], F32, name="xw%d" % k) for k in range(2)]
+        nc.vector.tensor_copy(tg[0], ta[:].indirect(lists[0][:]))
+        nc.vector.scalar_tensor_tensor(xw[0][:], tg[0], 1.0, ew[0][:], ALU.mult, ALU.mult, accum_out=xsums[0][:])
+        sig = sb.tile([P, 2], F32, name="sig", tag="xw0")
+        nc.vector.reciprocal(sig[:], den[:])
+        nc.vector.tensor_copy(tg[1], ta[:].indirect(lists[1][:]))
+        nc.vector.scalar_tensor_tensor(xw[1][:], tg[1], 1.0, ew[1][:], ALU.mult, ALU.mult, accum_out=xsums[1][:])
 
-        slope = column("slope")
-        nc.scalar.activation(slope[:], rest[:], ACT.Copy, scale=beta_t[:])
-        mix1 = column("mix1", 2)
-        nc.scalar.activation(mix1[:], one_zero[:], ACT.Identity, bias=slope[:])
-        grad = column("grad")
-        nc.scalar.activation(grad[:], capped[:], ACT.Copy, scale=slope[:])
-        mix2 = column("mix2", 2)
-        nc.scalar.activation(mix2[:], mix1[:], ACT.Identity, scale=-1.0, bias=1.0)
         mean1 = column("mean1")
         nc.scalar.activation(mean1[:], xsums[0][:], ACT.Copy, scale=inv[:, 0:1])
+        beta_mean1 = column("beta_mean1")
+        nc.scalar.activation(beta_mean1[:], mean1[:], ACT.Copy, scale=beta_t[:])
+        per_x2 = column("per_x2")
+        nc.scalar.activation(per_x2[:], neg_beta_inv2[:], ACT.Copy, scale=sig[:, 0:1])
         factor = column("factor", 2)
-        nc.scalar.activation(factor[:], inv[:], ACT.Copy, scale=grad[:])
-        per_x2 = column("per_x2", 2)
-        nc.scalar.activation(per_x2[:], mix2[:], ACT.Copy, scale=inv[:, 1:2])
-        from_x1 = column("from_x1", 2)
-        nc.scalar.activation(from_x1[:], mix1[:], ACT.Copy, scale=mean1[:])
+        nc.scalar.activation(factor[:], gain[:], ACT.Copy, scale=sig[:, 1:2])
+        from_x1 = column("from_x1")
+        nc.scalar.activation(from_x1[:], beta_mean1[:], ACT.Identity, scale=sig[:, 0:1], bias=mean1[:])
         neg_factor2 = column("neg_factor2")
         nc.scalar.activation(neg_factor2[:], factor[:, 1:2], ACT.Copy, scale=-1.0)
-        centre = column("centre", 2)
-        nc.vector.scalar_tensor_tensor(centre[:], per_x2[:], xsums[1][:], from_x1[:], ALU.mult, ALU.add)
-
-        placed = [sb.tile([P, V], F32, name="placed%d" % k) for k in range(2)]
-        for k in range(2):
-            for c in range(CHUNKS):
-                nc.vector.memset(placed[k][:, c * N : (c + 1) * N], 0.0)
+        centre1 = column("centre1")
+        nc.vector.tensor_scalar(centre1[:], xsums[1][:], per_x2[:], from_x1[:], ALU.mult, ALU.add)
 
         turned = []
         for c in range(CHUNKS):
@@ -189,11 +211,15 @@ def tile_attend_hvodds_heads_kernel(tc, hid, voc_words, voc_scales, sw, sw2, sav
             turned.append(bank)
 
         h = [sb.tile([P, I], F32, name="h%d" % k) for k in range(2)]
-        nc.vector.tensor_scalar(h[0][:], tg[0][:], centre[:, 0:1], factor[:, 0:1], ALU.subtract, ALU.mult)
+        nc.vector.tensor_scalar(h[0][:], tg[0], centre1[:], factor[:, 0:1], ALU.subtract, ALU.mult)
         nc.vector.tensor_tensor(placed[0][:].indirect(lists[0][:]), ew[0][:], h[0][:], ALU.mult)
         shift2 = column("shift2")
-        nc.scalar.activation(shift2[:], centre[:, 1:2], ACT.Copy, scale=factor[:, 1:2])
-        nc.scalar.activation(h[1][:], tg[1][:], ACT.Identity, scale=neg_factor2[:], bias=shift2[:])
+        common = column("common")
+        nc.scalar.activation(common[:], mean1[:], ACT.Identity, scale=-1.0, bias=centre1[:])
+        centre2 = column("centre2")
+        nc.scalar.activation(centre2[:], xsums[1][:], ACT.Identity, scale=inv[:, 1:2], bias=common[:])
+        nc.scalar.activation(shift2[:], centre2[:], ACT.Copy, scale=neg_factor2[:])
+        nc.scalar.activation(h[1][:], tg[1], ACT.Identity, scale=factor[:, 1:2], bias=shift2[:])
         nc.vector.tensor_tensor(placed[1][:].indirect(lists[1][:]), ew[1][:], h[1][:], ALU.mult)
 
         staged = []
@@ -218,8 +244,10 @@ def tile_attend_hvodds_heads_kernel(tc, hid, voc_words, voc_scales, sw, sw2, sav
                 turn_back(c - 1)
         turn_back(CHUNKS - 1)
 
-        for c in range(CHUNKS):
-            cols = slice(c * N, (c + 1) * N)
-            res = sb.tile([P, N], F32, name="res%d" % c)
-            nc.vector.tensor_tensor(res[:], partial[c][:].rearrange("p b v -> p (b v)"), placed[1][:, cols], ALU.add)
-            nc.sync.dma_start(out=out[:, cols], in_=res[:])
+        for first, last in OUT_PIECES:
+            c = first // N
+            res = sb.tile([P, last - first], F32, name="res%d" % first)
+            nc.vector.tensor_tensor(
+                res[:], partial[c][:].rearrange("p b v -> p (b v)")[:, first - c * N : last - c * N], placed[1][:, first:last], ALU.add
+            )
+            nc.sync.dma_start(out=out[:, first:last], in_=res[:])

@@ -23,7 +23,6 @@ N = 512
 CHUNKS = V // N
 BLOCKS = N // P
 OUT_SCALE = 256.0
-W_CAP = 1e30
 TA_BANKS = ("high0", "high1", "low0", "low1")
 OUT_PIECES = ((0, 512), (512, 1024), (1024, 1536), (1536, 1792), (1792, 2048))
 
@@ -37,21 +36,22 @@ def tile_attend_hvodds_heads_kernel(tc, hid, voc_words, voc_scales, sw, sw2, sav
         def column(name, width=1):
             return sb.tile([P, width], F32, name=name)
 
-        zero_one = column("zero_one", 2)
-        nc.gpsimd.memset(zero_one[:, 0:1], 0.0)
-        nc.gpsimd.memset(zero_one[:, 1:2], 1.0)
-        signs = column("signs", 2)
-        nc.scalar.activation(signs[:], zero_one[:], ACT.Identity, scale=-2.0, bias=1.0)
-
+        ident = sb.tile([P, P], F32, name="ident")
+        make_identity(nc, ident[:])
         raw = [sb.tile([P, PACK, Q], F32, name="raw%d" % k) for k in range(2)]
         nc.sync.dma_start(out=raw[0][:], in_=hid.rearrange("(p j) q -> p j q", j=PACK))
         landed = sb.tile([P, N // 4], I32, name="landed")
         for quad in range(4):
-            queue = nc.gpsimd if quad < 2 else nc.sync
-            queue.dma_start(
+            nc.scalar.dma_start(
                 out=landed[32 * quad : 32 * quad + 16, :],
                 in_=voc_scales[0, 4 * quad : 4 * quad + 4, :].rearrange("r (c n) -> c r n", c=CHUNKS).bitcast(I32),
             )
+        zero_one = column("zero_one", 2)
+        nc.vector.memset(zero_one[:, 0:1], 0.0)
+        nc.vector.memset(zero_one[:, 1:2], 1.0)
+        out_signs = column("out_signs", 2)
+        nc.scalar.activation(out_signs[:], zero_one[:], ACT.Identity, scale=-2.0 * OUT_SCALE, bias=OUT_SCALE)
+
         planes = sb.tile([P, N], U8, name="planes", align_bytes=64)
         nc.vector.memset(planes[:].bitcast(I32), 0)
         placed = [sb.tile([P, V], F32, name="placed%d" % k) for k in range(2)]
@@ -82,9 +82,6 @@ def tile_attend_hvodds_heads_kernel(tc, hid, voc_words, voc_scales, sw, sw2, sav
         nc.sync.dma_start(out=beta_t[:], in_=beta)
         base_t = sb.tile([P, V], F32, name="base_t")
         nc.sync.dma_start(out=base_t[:], in_=base)
-
-        ident = sb.tile([P, P], F32, name="ident")
-        make_identity(nc, ident[:])
 
         def interleave(k, engine_copy):
             grouped = sb.tile([P, Q, PACK], BF16, name="grouped%d" % k, align_bytes=64)
@@ -143,12 +140,12 @@ def tile_attend_hvodds_heads_kernel(tc, hid, voc_words, voc_scales, sw, sw2, sav
             nc.vector.tensor_copy(picked[:], a[:].indirect(lists[k][:]))
             nc.scalar.activation(px[k], picked[:], ACT.Exp, bias=neg_max[:])
 
-        exp_saved = column("exp_saved")
-        nc.scalar.activation(exp_saved[:], saved_t[:], ACT.Exp)
-        betas = column("betas", 2)
-        nc.scalar.activation(betas[:], signs[:], ACT.Copy, scale=beta_t[:])
-        beta_out = column("beta_out")
-        nc.scalar.activation(beta_out[:], beta_t[:], ACT.Copy, scale=OUT_SCALE)
+        neg_beta = column("neg_beta")
+        nc.scalar.activation(neg_beta[:], beta_t[:], ACT.Copy, scale=-1.0)
+        beta_saved = column("beta_saved")
+        nc.scalar.activation(beta_saved[:], saved_t[:], ACT.Copy, scale=beta_t[:])
+        neg_beta_saved = column("neg_beta_saved")
+        nc.scalar.activation(neg_beta_saved[:], saved_t[:], ACT.Copy, scale=neg_beta[:])
 
         sums = column("sums", 2)
         ew = []
@@ -162,45 +159,39 @@ def tile_attend_hvodds_heads_kernel(tc, hid, voc_words, voc_scales, sw, sw2, sav
         inv = column("inv", 2)
         nc.vector.reciprocal(inv[:], sums[:])
 
-        lifted = column("lifted", 2)
-        nc.scalar.activation(lifted[:], sums[:, 1:2].to_broadcast([P, 2]), ACT.Copy, scale=exp_saved[:])
-        odds = column("odds", 2)
-        nc.scalar.activation(odds[:], lifted[:], ACT.Copy, scale=inv[:, 0:1])
-        powers = column("powers", 2)
-        nc.gpsimd.tensor_tensor(powers[:], odds[:], betas[:], ALU.pow)
-        gain = column("gain", 2)
-        nc.scalar.activation(gain[:, 0:1], inv[:, 0:1], ACT.Copy, scale=beta_out[:])
-        neg_beta_inv2 = column("neg_beta_inv2")
-        nc.scalar.activation(neg_beta_inv2[:], inv[:, 1:2], ACT.Copy, scale=betas[:, 1:2])
-        nc.scalar.activation(gain[:, 1:2], neg_beta_inv2[:], ACT.Copy, scale=OUT_SCALE)
-        den = column("den", 2)
-        nc.scalar.activation(den[:], powers[:], ACT.Identity, bias=1.0)
+        logs = column("logs", 2)
+        nc.scalar.activation(logs[:, 1:2], sums[:, 1:2], ACT.Ln)
+        nc.scalar.activation(logs[:, 0:1], inv[:, 0:1], ACT.Ln)
+        log_odds = column("log_odds")
+        nc.scalar.activation(log_odds[:], logs[:, 0:1], ACT.Identity, bias=logs[:, 1:2])
+        rest = column("rest")
+        nc.scalar.activation(rest[:], log_odds[:], ACT.Sigmoid, scale=neg_beta[:], bias=neg_beta_saved[:])
+        sigma = column("sigma")
+        nc.scalar.activation(sigma[:], log_odds[:], ACT.Sigmoid, scale=beta_t[:], bias=beta_saved[:])
 
         pair = sb.tile([P, 2, I], F32, name="tg", tag="pair")
         tg = [pair[:, k, :] for k in range(2)]
         xsums = [column("xsum%d" % k) for k in range(2)]
         xw = [sb.tile([P, I], F32, name="xw%d" % k) for k in range(2)]
         nc.vector.tensor_copy(tg[0], ta[:].indirect(lists[0][:]))
-        nc.vector.scalar_tensor_tensor(xw[0][:], tg[0], 1.0, ew[0][:], ALU.mult, ALU.mult, accum_out=xsums[0][:])
-        sig = sb.tile([P, 2], F32, name="sig", tag="xw0")
-        nc.vector.reciprocal(sig[:], den[:])
+        beta_inv = column("beta_inv", 2)
+        nc.vector.tensor_scalar(beta_inv[:], inv[:], beta_t[:], None, ALU.mult)
+        gain = column("gain", 2)
+        nc.vector.scalar_tensor_tensor(gain[:], inv[:], beta_t[:], out_signs[:], ALU.mult, ALU.mult)
         nc.vector.tensor_copy(tg[1], ta[:].indirect(lists[1][:]))
-        nc.vector.scalar_tensor_tensor(xw[1][:], tg[1], 1.0, ew[1][:], ALU.mult, ALU.mult, accum_out=xsums[1][:])
+        for k in range(2):
+            nc.vector.scalar_tensor_tensor(xw[k][:], tg[k], 1.0, ew[k][:], ALU.mult, ALU.mult, accum_out=xsums[k][:])
 
-        mean1 = column("mean1")
-        nc.scalar.activation(mean1[:], xsums[0][:], ACT.Copy, scale=inv[:, 0:1])
-        beta_mean1 = column("beta_mean1")
-        nc.scalar.activation(beta_mean1[:], mean1[:], ACT.Copy, scale=beta_t[:])
-        per_x2 = column("per_x2")
-        nc.scalar.activation(per_x2[:], neg_beta_inv2[:], ACT.Copy, scale=sig[:, 0:1])
+        per_x1 = column("per_x1")
+        nc.scalar.activation(per_x1[:], beta_inv[:, 0:1], ACT.Identity, scale=rest[:], bias=inv[:, 0:1])
+        slope = column("slope", 2)
+        nc.scalar.activation(slope[:], beta_inv[:], ACT.Copy, scale=rest[:])
         factor = column("factor", 2)
-        nc.scalar.activation(factor[:], gain[:], ACT.Copy, scale=sig[:, 1:2])
+        nc.scalar.activation(factor[:], gain[:], ACT.Copy, scale=sigma[:])
         from_x1 = column("from_x1")
-        nc.scalar.activation(from_x1[:], beta_mean1[:], ACT.Identity, scale=sig[:, 0:1], bias=mean1[:])
-        neg_factor2 = column("neg_factor2")
-        nc.scalar.activation(neg_factor2[:], factor[:, 1:2], ACT.Copy, scale=-1.0)
-        centre1 = column("centre1")
-        nc.vector.tensor_scalar(centre1[:], xsums[1][:], per_x2[:], from_x1[:], ALU.mult, ALU.add)
+        nc.scalar.activation(from_x1[:], xsums[0][:], ACT.Copy, scale=per_x1[:])
+        neg_centre1 = column("neg_centre1")
+        nc.vector.tensor_scalar(neg_centre1[:], xsums[1][:], slope[:, 1:2], from_x1[:], ALU.mult, ALU.subtract)
 
         turned = []
         for c in range(CHUNKS):
@@ -211,14 +202,18 @@ def tile_attend_hvodds_heads_kernel(tc, hid, voc_words, voc_scales, sw, sw2, sav
             turned.append(bank)
 
         h = [sb.tile([P, I], F32, name="h%d" % k) for k in range(2)]
-        nc.vector.tensor_scalar(h[0][:], tg[0], centre1[:], factor[:, 0:1], ALU.subtract, ALU.mult)
+        nc.vector.tensor_scalar(h[0][:], tg[0], neg_centre1[:], factor[:, 0:1], ALU.add, ALU.mult)
         nc.vector.tensor_tensor(placed[0][:].indirect(lists[0][:]), ew[0][:], h[0][:], ALU.mult)
+        neg_per_x2 = column("neg_per_x2")
+        nc.scalar.activation(neg_per_x2[:], inv[:, 1:2], ACT.Identity, scale=-1.0, bias=slope[:, 1:2])
+        neg_slope1 = column("neg_slope1")
+        nc.scalar.activation(neg_slope1[:], slope[:, 0:1], ACT.Copy, scale=-1.0)
+        neg_part = column("neg_part")
+        nc.scalar.activation(neg_part[:], xsums[0][:], ACT.Copy, scale=neg_slope1[:])
+        neg_centre2 = column("neg_centre2")
+        nc.scalar.activation(neg_centre2[:], xsums[1][:], ACT.Identity, scale=neg_per_x2[:], bias=neg_part[:])
         shift2 = column("shift2")
-        common = column("common")
-        nc.scalar.activation(common[:], mean1[:], ACT.Identity, scale=-1.0, bias=centre1[:])
-        centre2 = column("centre2")
-        nc.scalar.activation(centre2[:], xsums[1][:], ACT.Identity, scale=inv[:, 1:2], bias=common[:])
-        nc.scalar.activation(shift2[:], centre2[:], ACT.Copy, scale=neg_factor2[:])
+        nc.scalar.activation(shift2[:], neg_centre2[:], ACT.Copy, scale=factor[:, 1:2])
         nc.scalar.activation(h[1][:], tg[1], ACT.Identity, scale=factor[:, 1:2], bias=shift2[:])
         nc.vector.tensor_tensor(placed[1][:].indirect(lists[1][:]), ew[1][:], h[1][:], ALU.mult)
 

@@ -23,8 +23,8 @@ N = 512
 CHUNKS = V // N
 BLOCKS = N // P
 OUT_SCALE = 256.0
-TA_BANKS = ("high0", "high1", "low0", "low1")
-OUT_PIECES = ((0, 512), (512, 1024), (1024, 1536), (1536, 1792), (1792, 2048))
+DIRECT = 256
+TURNED_BLOCKS = (4, 4, 4, 2)
 
 
 def tile_attend_hvodds_heads_kernel(tc, hid, voc_words, voc_scales, sw, sw2, saved, beta, dhid, base, offs, offs2, out):
@@ -42,10 +42,11 @@ def tile_attend_hvodds_heads_kernel(tc, hid, voc_words, voc_scales, sw, sw2, sav
         nc.sync.dma_start(out=raw[0][:], in_=hid.rearrange("(p j) q -> p j q", j=PACK))
         landed = sb.tile([P, N // 4], I32, name="landed")
         for quad in range(4):
-            nc.scalar.dma_start(
+            nc.sync.dma_start(
                 out=landed[32 * quad : 32 * quad + 16, :],
                 in_=voc_scales[0, 4 * quad : 4 * quad + 4, :].rearrange("r (c n) -> c r n", c=CHUNKS).bitcast(I32),
             )
+        nc.sync.dma_start(out=raw[1][:], in_=dhid.rearrange("(p j) q -> p j q", j=PACK))
         zero_one = column("zero_one", 2)
         nc.vector.memset(zero_one[:, 0:1], 0.0)
         nc.vector.memset(zero_one[:, 1:2], 1.0)
@@ -64,8 +65,6 @@ def tile_attend_hvodds_heads_kernel(tc, hid, voc_words, voc_scales, sw, sw2, sav
             t = sb.tile([P, N], U32, name="words%d" % c, align_bytes=64)
             nc.sync.dma_start(out=t[:].bitcast(I32), in_=words_flat[:, PACK * N * c : PACK * N * (c + 1)].bitcast(I32))
             words.append(t[:])
-            if c == 0:
-                nc.sync.dma_start(out=raw[1][:], in_=dhid.rearrange("(p j) q -> p j q", j=PACK))
         lists = []
         for name, src in (("list1", offs), ("list2", offs2)):
             t = sb.tile([P, I // 16], U16, name=name)
@@ -122,7 +121,7 @@ def tile_attend_hvodds_heads_kernel(tc, hid, voc_words, voc_scales, sw, sw2, sav
                 accum_out=chunk_max[:, c : c + 1],
             )
         for c in range(CHUNKS):
-            bank = score(*quantised[1], c, TA_BANKS[c])
+            bank = score(*quantised[1], c, "low%d" % c)
             nc.scalar.copy(out=ta[:, c * N : (c + 1) * N], in_=bank[:])
         weights = []
         for k in range(2):
@@ -160,43 +159,45 @@ def tile_attend_hvodds_heads_kernel(tc, hid, voc_words, voc_scales, sw, sw2, sav
         nc.vector.reciprocal(inv[:], sums[:])
 
         logs = column("logs", 2)
-        nc.scalar.activation(logs[:, 1:2], sums[:, 1:2], ACT.Ln)
-        nc.scalar.activation(logs[:, 0:1], inv[:, 0:1], ACT.Ln)
+        for k in range(2):
+            nc.scalar.activation(logs[:, k : k + 1], sums[:, k : k + 1], ACT.Ln)
         log_odds = column("log_odds")
-        nc.scalar.activation(log_odds[:], logs[:, 0:1], ACT.Identity, bias=logs[:, 1:2])
-        rest = column("rest")
-        nc.scalar.activation(rest[:], log_odds[:], ACT.Sigmoid, scale=neg_beta[:], bias=neg_beta_saved[:])
-        sigma = column("sigma")
-        nc.scalar.activation(sigma[:], log_odds[:], ACT.Sigmoid, scale=beta_t[:], bias=beta_saved[:])
+        nc.scalar.activation(log_odds[:], logs[:, 0:1], ACT.Identity, scale=-1.0, bias=logs[:, 1:2])
 
         pair = sb.tile([P, 2, I], F32, name="tg", tag="pair")
         tg = [pair[:, k, :] for k in range(2)]
         xsums = [column("xsum%d" % k) for k in range(2)]
         xw = [sb.tile([P, I], F32, name="xw%d" % k) for k in range(2)]
         nc.vector.tensor_copy(tg[0], ta[:].indirect(lists[0][:]))
-        beta_inv = column("beta_inv", 2)
-        nc.vector.tensor_scalar(beta_inv[:], inv[:], beta_t[:], None, ALU.mult)
+        beta_inv2 = column("beta_inv2")
+        nc.vector.tensor_scalar(beta_inv2[:], inv[:, 1:2], beta_t[:], None, ALU.mult)
         gain = column("gain", 2)
         nc.vector.scalar_tensor_tensor(gain[:], inv[:], beta_t[:], out_signs[:], ALU.mult, ALU.mult)
+        nc.vector.scalar_tensor_tensor(xw[0][:], tg[0], 1.0, ew[0][:], ALU.mult, ALU.mult, accum_out=xsums[0][:])
         nc.vector.tensor_copy(tg[1], ta[:].indirect(lists[1][:]))
-        for k in range(2):
-            nc.vector.scalar_tensor_tensor(xw[k][:], tg[k], 1.0, ew[k][:], ALU.mult, ALU.mult, accum_out=xsums[k][:])
+        mean1 = column("mean1")
+        nc.vector.tensor_tensor(mean1[:], xsums[0][:], inv[:, 0:1], ALU.mult)
+        beta_mean1 = column("beta_mean1")
+        nc.vector.tensor_scalar(beta_mean1[:], xsums[0][:], inv[:, 0:1], beta_t[:], ALU.mult, ALU.mult)
+        nc.vector.scalar_tensor_tensor(xw[1][:], tg[1], 1.0, ew[1][:], ALU.mult, ALU.mult, accum_out=xsums[1][:])
 
-        per_x1 = column("per_x1")
-        nc.scalar.activation(per_x1[:], beta_inv[:, 0:1], ACT.Identity, scale=rest[:], bias=inv[:, 0:1])
-        slope = column("slope", 2)
-        nc.scalar.activation(slope[:], beta_inv[:], ACT.Copy, scale=rest[:])
+        rest = column("rest")
+        nc.scalar.activation(rest[:], log_odds[:], ACT.Sigmoid, scale=neg_beta[:], bias=neg_beta_saved[:])
+        sigma = column("sigma")
+        nc.scalar.activation(sigma[:], log_odds[:], ACT.Sigmoid, scale=beta_t[:], bias=beta_saved[:])
+        slope2 = column("slope2")
+        nc.scalar.activation(slope2[:], beta_inv2[:], ACT.Copy, scale=rest[:])
+        from_x1 = column("from_x1")
+        nc.scalar.activation(from_x1[:], beta_mean1[:], ACT.Identity, scale=rest[:], bias=mean1[:])
         factor = column("factor", 2)
         nc.scalar.activation(factor[:], gain[:], ACT.Copy, scale=sigma[:])
-        from_x1 = column("from_x1")
-        nc.scalar.activation(from_x1[:], xsums[0][:], ACT.Copy, scale=per_x1[:])
         neg_centre1 = column("neg_centre1")
-        nc.vector.tensor_scalar(neg_centre1[:], xsums[1][:], slope[:, 1:2], from_x1[:], ALU.mult, ALU.subtract)
+        nc.vector.tensor_scalar(neg_centre1[:], xsums[1][:], slope2[:], from_x1[:], ALU.mult, ALU.subtract)
 
         turned = []
         for c in range(CHUNKS):
-            bank = psum.tile([P, BLOCKS, P], F32, name="turned%d" % c, tag="low%d" % c)
-            for b in range(BLOCKS):
+            bank = psum.tile([P, TURNED_BLOCKS[c], P], F32, name="turned%d" % c, tag="low%d" % c)
+            for b in range(TURNED_BLOCKS[c]):
                 cols = slice(c * N + b * P, c * N + (b + 1) * P)
                 nc.tensor.matmul(bank[:, b, :], base_t[:, cols], ident[:], start=(b == 0), stop=False, is_transpose=True)
             turned.append(bank)
@@ -204,14 +205,12 @@ def tile_attend_hvodds_heads_kernel(tc, hid, voc_words, voc_scales, sw, sw2, sav
         h = [sb.tile([P, I], F32, name="h%d" % k) for k in range(2)]
         nc.vector.tensor_scalar(h[0][:], tg[0], neg_centre1[:], factor[:, 0:1], ALU.add, ALU.mult)
         nc.vector.tensor_tensor(placed[0][:].indirect(lists[0][:]), ew[0][:], h[0][:], ALU.mult)
-        neg_per_x2 = column("neg_per_x2")
-        nc.scalar.activation(neg_per_x2[:], inv[:, 1:2], ACT.Identity, scale=-1.0, bias=slope[:, 1:2])
-        neg_slope1 = column("neg_slope1")
-        nc.scalar.activation(neg_slope1[:], slope[:, 0:1], ACT.Copy, scale=-1.0)
-        neg_part = column("neg_part")
-        nc.scalar.activation(neg_part[:], xsums[0][:], ACT.Copy, scale=neg_slope1[:])
+        mean2 = column("mean2")
+        nc.scalar.activation(mean2[:], xsums[1][:], ACT.Copy, scale=inv[:, 1:2])
+        neg_common = column("neg_common")
+        nc.scalar.activation(neg_common[:], neg_centre1[:], ACT.Identity, bias=mean1[:])
         neg_centre2 = column("neg_centre2")
-        nc.scalar.activation(neg_centre2[:], xsums[1][:], ACT.Identity, scale=neg_per_x2[:], bias=neg_part[:])
+        nc.scalar.activation(neg_centre2[:], mean2[:], ACT.Identity, scale=-1.0, bias=neg_common[:])
         shift2 = column("shift2")
         nc.scalar.activation(shift2[:], neg_centre2[:], ACT.Copy, scale=factor[:, 1:2])
         nc.scalar.activation(h[1][:], tg[1], ACT.Identity, scale=factor[:, 1:2], bias=shift2[:])
@@ -221,28 +220,33 @@ def tile_attend_hvodds_heads_kernel(tc, hid, voc_words, voc_scales, sw, sw2, sav
         partial = []
 
         def turn_back(c):
-            bank = psum.tile([P, BLOCKS, P], F32, name="partial%d" % c, tag="high%d" % c)
-            for b in range(BLOCKS):
+            bank = psum.tile([P, TURNED_BLOCKS[c], P], F32, name="partial%d" % c, tag="high%d" % c)
+            for b in range(TURNED_BLOCKS[c]):
                 nc.tensor.transpose(bank[:, b, :], staged[c][:, b, :], ident[:])
             partial.append(bank)
 
         for c in range(CHUNKS):
-            for b in range(BLOCKS):
+            blocks = TURNED_BLOCKS[c]
+            for b in range(blocks):
                 cols = slice(c * N + b * P, c * N + (b + 1) * P)
                 nc.tensor.matmul(
-                    turned[c][:, b, :], placed[0][:, cols], ident[:], start=False, stop=(b == BLOCKS - 1), is_transpose=True
+                    turned[c][:, b, :], placed[0][:, cols], ident[:], start=False, stop=(b == blocks - 1), is_transpose=True
                 )
-            t = sb.tile([P, BLOCKS, P], F32, name="staged%d" % c)
+            t = sb.tile([P, blocks, P], F32, name="staged%d" % c)
             nc.scalar.copy(out=t[:], in_=turned[c][:])
             staged.append(t)
             if c > 0:
                 turn_back(c - 1)
         turn_back(CHUNKS - 1)
 
-        for first, last in OUT_PIECES:
-            c = first // N
-            res = sb.tile([P, last - first], F32, name="res%d" % first)
-            nc.vector.tensor_tensor(
-                res[:], partial[c][:].rearrange("p b v -> p (b v)")[:, first - c * N : last - c * N], placed[1][:, first:last], ALU.add
-            )
-            nc.sync.dma_start(out=out[:, first:last], in_=res[:])
+        def finish(first, width, part):
+            res = sb.tile([P, width], F32, name="res%d" % first)
+            nc.vector.tensor_tensor(res[:], part, placed[1][:, first : first + width], ALU.add)
+            nc.sync.dma_start(out=out[:, first : first + width], in_=res[:])
+
+        for c in range(CHUNKS):
+            finish(c * N, TURNED_BLOCKS[c] * P, partial[c][:].rearrange("p b v -> p (b v)"))
+            if c == 0:
+                direct = sb.tile([P, DIRECT], F32, name="direct")
+                nc.vector.tensor_tensor(direct[:], base_t[:, V - DIRECT :], placed[0][:, V - DIRECT :], ALU.add)
+                finish(V - DIRECT, DIRECT, direct[:])

from contextlib import ExitStack

import concourse.mybir as mybir
from concourse.masks import make_identity

D, V, Q, I = 512, 2048, 128, 512
FLOPS = 2 * 2 * D * V * Q

F32 = mybir.dt.float32
BF16 = mybir.dt.bfloat16
I32 = mybir.dt.int32
U32 = mybir.dt.uint32
U16 = mybir.dt.uint16
U8 = mybir.dt.uint8
FP8X4 = mybir.dt.float8_e4m3fn_x4
ALU = mybir.AluOpType
ACT = mybir.ActivationFunctionType
AX = mybir.AxisListType

P = 128
PACK = 4
N = 512
CHUNKS = V // N
BLOCKS = N // P
OUT_SCALE = 256.0
DIRECT = 256
TURNED_BLOCKS = (4, 4, 4, 2)


def tile_attend_hvodds_heads_kernel(tc, hid, voc_words, voc_scales, sw, sw2, saved, beta, dhid, base, offs, offs2, out):
    nc = tc.nc
    with ExitStack() as ctx:
        sb = ctx.enter_context(tc.tile_pool(name="sb", bufs=1))
        psum = ctx.enter_context(tc.psum_pool(name="psum", bufs=1))

        def column(name, width=1):
            return sb.tile([P, width], F32, name=name)

        ident = sb.tile([P, P], F32, name="ident")
        make_identity(nc, ident[:])
        raw = [sb.tile([P, PACK, Q], F32, name="raw%d" % k) for k in range(2)]
        nc.sync.dma_start(out=raw[0][:], in_=hid.rearrange("(p j) q -> p j q", j=PACK))
        landed = sb.tile([P, N // 4], I32, name="landed")
        for quad in range(4):
            nc.sync.dma_start(
                out=landed[32 * quad : 32 * quad + 16, :],
                in_=voc_scales[0, 4 * quad : 4 * quad + 4, :].rearrange("r (c n) -> c r n", c=CHUNKS).bitcast(I32),
            )
        nc.sync.dma_start(out=raw[1][:], in_=dhid.rearrange("(p j) q -> p j q", j=PACK))
        zero_one = column("zero_one", 2)
        nc.vector.memset(zero_one[:, 0:1], 0.0)
        nc.vector.memset(zero_one[:, 1:2], 1.0)
        out_signs = column("out_signs", 2)
        nc.scalar.activation(out_signs[:], zero_one[:], ACT.Identity, scale=-2.0 * OUT_SCALE, bias=OUT_SCALE)

        planes = sb.tile([P, N], U8, name="planes", align_bytes=64)
        nc.vector.memset(planes[:].bitcast(I32), 0)
        placed = [sb.tile([P, V], F32, name="placed%d" % k) for k in range(2)]
        for k in range(2):
            for c in range(CHUNKS):
                nc.vector.memset(placed[k][:, c * N : (c + 1) * N].bitcast(I32), 0)
        words_flat = voc_words[0].rearrange("p n t -> p (n t)")
        words = []
        for c in range(CHUNKS):
            t = sb.tile([P, N], U32, name="words%d" % c, align_bytes=64)
            nc.sync.dma_start(out=t[:].bitcast(I32), in_=words_flat[:, PACK * N * c : PACK * N * (c + 1)].bitcast(I32))
            words.append(t[:])
        lists = []
        for name, src in (("list1", offs), ("list2", offs2)):
            t = sb.tile([P, I // 16], U16, name=name)
            nc.sync.dma_start(t[:], src)
            lists.append(t)
        slot_weights = []
        for k, src in enumerate((sw, sw2)):
            t = column("slot_weights%d" % k, BLOCKS)
            nc.sync.dma_start(out=t[:], in_=src[0].rearrange("(n c) -> n c", c=BLOCKS))
            slot_weights.append(t)
        saved_t = column("saved_t")
        nc.sync.dma_start(out=saved_t[:], in_=saved)
        beta_t = column("beta_t")
        nc.sync.dma_start(out=beta_t[:], in_=beta)
        base_t = sb.tile([P, V], F32, name="base_t")
        nc.sync.dma_start(out=base_t[:], in_=base)

        def interleave(k, engine_copy):
            grouped = sb.tile([P, Q, PACK], BF16, name="grouped%d" % k, align_bytes=64)
            engine_copy(out=grouped[:], in_=raw[k][:].rearrange("p j q -> p q j"))
            return grouped

        def quantise(k, grouped):
            cw = sb.tile([P, Q], U32, name="codes%d" % k, align_bytes=64)
            sc = sb.tile([P, Q], U8, name="scales%d" % k, align_bytes=64)
            nc.vector.quantize_mx(out=cw[:].bitcast(FP8X4), scales=sc[:], in_=grouped[:].rearrange("p q j -> p (q j)"))
            return cw, sc

        def score(cw, sc, c, tag):
            bank = psum.tile([P, N], F32, name="score_" + tag, tag=tag)
            nc.tensor.matmul_mx(
                out=bank[:],
                lhsT=cw[:].bitcast(FP8X4),
                lhsT_scale=sc[:],
                rhs=words[c].bitcast(FP8X4),
                rhs_scale=planes[4 * c : P, :],
                start=True,
                stop=True,
            )
            return bank

        a = sb.tile([P, V], F32, name="a")
        ta = sb.tile([P, V], F32, name="ta")
        chunk_max = sb.tile([P, CHUNKS], F32, name="chunk_max")
        grouped = [interleave(0, nc.vector.tensor_copy), interleave(1, nc.scalar.copy)]
        for quad in range(4):
            rows = slice(32 * quad, 32 * quad + 16)
            nc.vector.tensor_copy(out=planes[rows, :].bitcast(I32), in_=landed[rows, :])
        quantised = [quantise(k, grouped[k]) for k in range(2)]
        for c in range(CHUNKS):
            bank = score(*quantised[0], c, "low%d" % c)
            nc.vector.tensor_scalar(
                out=a[:, c * N : (c + 1) * N], in0=bank[:], scalar1=1.0, scalar2=None, op0=ALU.mult, op1=ALU.max,
                accum_out=chunk_max[:, c : c + 1],
            )
        for c in range(CHUNKS):
            bank = score(*quantised[1], c, "low%d" % c)
            nc.scalar.copy(out=ta[:, c * N : (c + 1) * N], in_=bank[:])
        weights = []
        for k in range(2):
            bank = psum.tile([P, BLOCKS, P], F32, name="spread%d" % k, tag="high%d" % (2 + k))
            for b in range(BLOCKS):
                nc.tensor.transpose(bank[:, b, :], slot_weights[k][:, b : b + 1].to_broadcast([P, P]), ident[:])
            weights.append(bank[:].rearrange("p c n -> p n c"))
        neg_max = sb.tile([P, 1], F32, name="neg_max")
        nc.vector.tensor_reduce(out=neg_max[:], in_=chunk_max[:], axis=AX.X, op=ALU.max, negate=True)

        pair = sb.tile([P, 2, I], F32, name="px", tag="pair")
        px = [pair[:, k, :] for k in range(2)]
        for k in range(2):
            picked = sb.tile([P, I], F32, name="picked%d" % k)
            nc.vector.tensor_copy(picked[:], a[:].indirect(lists[k][:]))
            nc.scalar.activation(px[k], picked[:], ACT.Exp, bias=neg_max[:])

        neg_beta = column("neg_beta")
        nc.scalar.activation(neg_beta[:], beta_t[:], ACT.Copy, scale=-1.0)
        beta_saved = column("beta_saved")
        nc.scalar.activation(beta_saved[:], saved_t[:], ACT.Copy, scale=beta_t[:])
        neg_beta_saved = column("neg_beta_saved")
        nc.scalar.activation(neg_beta_saved[:], saved_t[:], ACT.Copy, scale=neg_beta[:])

        sums = column("sums", 2)
        ew = []
        for k in range(2):
            e = sb.tile([P, I], F32, name="ew%d" % k)
            nc.vector.scalar_tensor_tensor(
                e[:].rearrange("p (n c) -> p n c", c=BLOCKS), px[k].rearrange("p (n c) -> p n c", c=BLOCKS), 1.0, weights[k],
                ALU.mult, ALU.mult, accum_out=sums[:, k : k + 1],
            )
            ew.append(e)
        inv = column("inv", 2)
        nc.vector.reciprocal(inv[:], sums[:])

        logs = column("logs", 2)
        for k in range(2):
            nc.scalar.activation(logs[:, k : k + 1], sums[:, k : k + 1], ACT.Ln)
        log_odds = column("log_odds")
        nc.scalar.activation(log_odds[:], logs[:, 0:1], ACT.Identity, scale=-1.0, bias=logs[:, 1:2])

        pair = sb.tile([P, 2, I], F32, name="tg", tag="pair")
        tg = [pair[:, k, :] for k in range(2)]
        xsums = [column("xsum%d" % k) for k in range(2)]
        xw = [sb.tile([P, I], F32, name="xw%d" % k) for k in range(2)]
        nc.vector.tensor_copy(tg[0], ta[:].indirect(lists[0][:]))
        beta_inv2 = column("beta_inv2")
        nc.vector.tensor_scalar(beta_inv2[:], inv[:, 1:2], beta_t[:], None, ALU.mult)
        gain = column("gain", 2)
        nc.vector.scalar_tensor_tensor(gain[:], inv[:], beta_t[:], out_signs[:], ALU.mult, ALU.mult)
        nc.vector.scalar_tensor_tensor(xw[0][:], tg[0], 1.0, ew[0][:], ALU.mult, ALU.mult, accum_out=xsums[0][:])
        nc.vector.tensor_copy(tg[1], ta[:].indirect(lists[1][:]))
        mean1 = column("mean1")
        nc.vector.tensor_tensor(mean1[:], xsums[0][:], inv[:, 0:1], ALU.mult)
        beta_mean1 = column("beta_mean1")
        nc.vector.tensor_scalar(beta_mean1[:], xsums[0][:], inv[:, 0:1], beta_t[:], ALU.mult, ALU.mult)
        nc.vector.scalar_tensor_tensor(xw[1][:], tg[1], 1.0, ew[1][:], ALU.mult, ALU.mult, accum_out=xsums[1][:])

        rest = column("rest")
        nc.scalar.activation(rest[:], log_odds[:], ACT.Sigmoid, scale=neg_beta[:], bias=neg_beta_saved[:])
        sigma = column("sigma")
        nc.scalar.activation(sigma[:], log_odds[:], ACT.Sigmoid, scale=beta_t[:], bias=beta_saved[:])
        slope2 = column("slope2")
        nc.scalar.activation(slope2[:], beta_inv2[:], ACT.Copy, scale=rest[:])
        from_x1 = column("from_x1")
        nc.scalar.activation(from_x1[:], beta_mean1[:], ACT.Identity, scale=rest[:], bias=mean1[:])
        factor = column("factor", 2)
        nc.scalar.activation(factor[:], gain[:], ACT.Copy, scale=sigma[:])
        neg_centre1 = column("neg_centre1")
        nc.vector.tensor_scalar(neg_centre1[:], xsums[1][:], slope2[:], from_x1[:], ALU.mult, ALU.subtract)

        turned = []
        for c in range(CHUNKS):
            bank = psum.tile([P, TURNED_BLOCKS[c], P], F32, name="turned%d" % c, tag="low%d" % c)
            for b in range(TURNED_BLOCKS[c]):
                cols = slice(c * N + b * P, c * N + (b + 1) * P)
                nc.tensor.matmul(bank[:, b, :], base_t[:, cols], ident[:], start=(b == 0), stop=False, is_transpose=True)
            turned.append(bank)

        h = [sb.tile([P, I], F32, name="h%d" % k) for k in range(2)]
        nc.vector.tensor_scalar(h[0][:], tg[0], neg_centre1[:], factor[:, 0:1], ALU.add, ALU.mult)
        nc.vector.tensor_tensor(placed[0][:].indirect(lists[0][:]), ew[0][:], h[0][:], ALU.mult)
        mean2 = column("mean2")
        nc.scalar.activation(mean2[:], xsums[1][:], ACT.Copy, scale=inv[:, 1:2])
        neg_common = column("neg_common")
        nc.scalar.activation(neg_common[:], neg_centre1[:], ACT.Identity, bias=mean1[:])
        neg_centre2 = column("neg_centre2")
        nc.scalar.activation(neg_centre2[:], mean2[:], ACT.Identity, scale=-1.0, bias=neg_common[:])
        shift2 = column("shift2")
        nc.scalar.activation(shift2[:], neg_centre2[:], ACT.Copy, scale=factor[:, 1:2])
        nc.scalar.activation(h[1][:], tg[1], ACT.Identity, scale=factor[:, 1:2], bias=shift2[:])
        nc.vector.tensor_tensor(placed[1][:].indirect(lists[1][:]), ew[1][:], h[1][:], ALU.mult)

        staged = []
        partial = []

        def turn_back(c):
            bank = psum.tile([P, TURNED_BLOCKS[c], P], F32, name="partial%d" % c, tag="high%d" % c)
            for b in range(TURNED_BLOCKS[c]):
                nc.tensor.transpose(bank[:, b, :], staged[c][:, b, :], ident[:])
            partial.append(bank)

        for c in range(CHUNKS):
            blocks = TURNED_BLOCKS[c]
            for b in range(blocks):
                cols = slice(c * N + b * P, c * N + (b + 1) * P)
                nc.tensor.matmul(
                    turned[c][:, b, :], placed[0][:, cols], ident[:], start=False, stop=(b == blocks - 1), is_transpose=True
                )
            t = sb.tile([P, blocks, P], F32, name="staged%d" % c)
            nc.scalar.copy(out=t[:], in_=turned[c][:])
            staged.append(t)
            if c > 0:
                turn_back(c - 1)
        turn_back(CHUNKS - 1)

        def finish(first, width, part):
            res = sb.tile([P, width], F32, name="res%d" % first)
            nc.vector.tensor_tensor(res[:], part, placed[1][:, first : first + width], ALU.add)
            nc.sync.dma_start(out=out[:, first : first + width], in_=res[:])

        for c in range(CHUNKS):
            finish(c * N, TURNED_BLOCKS[c] * P, partial[c][:].rearrange("p b v -> p (b v)"))
            if c == 0:
                direct = sb.tile([P, DIRECT], F32, name="direct")
                nc.vector.tensor_tensor(direct[:], base_t[:, V - DIRECT :], placed[0][:, V - DIRECT :], ALU.add)
                finish(V - DIRECT, DIRECT, direct[:])
